import numpy as np
import ml_dtypes


def mxq(x, axis, fmt="e4m3"):
    dtype, down = {"e4m3": (ml_dtypes.float8_e4m3fn, 7), "e5m2": (ml_dtypes.float8_e5m2, 14)}[fmt]
    v = np.moveaxis(np.asarray(x, np.float32).astype(ml_dtypes.bfloat16).astype(np.float64), axis, -1)
    blocks = v.reshape(v.shape[:-1] + (-1, 32))
    amax = np.abs(blocks).max(-1, keepdims=True)
    byte = np.maximum(np.where(amax > 0, np.frexp(amax)[1] - 1 + 127, 0) - down, 1)
    scale = np.exp2(byte - 127.0)
    codes = (blocks / scale).astype(np.float32).astype(dtype).astype(np.float64)
    return np.moveaxis((codes * scale).reshape(v.shape), -1, axis)


WIDE = False


def mx_kscale(k):
    if not WIDE:
        return np.ones(k)
    levels = np.array([10, -10, 5, -5, 0])
    if k % 512:
        return np.exp2(np.random.permutation(np.resize(levels, k // 32))).repeat(32)
    a = np.empty((k // 512, 16))
    for p in range(k // 512):
        a[p, :8] = np.random.permutation(np.resize(levels, 8))
        for g in range(8):
            far = levels[np.abs(levels - a[p, g]) >= 10]
            a[p, g + 8] = far[np.random.randint(len(far))]
    return np.exp2(a.ravel()).repeat(32)


def f64(x):
    return np.asarray(x).astype(np.float64)


def striped(idx):
    return np.tile(idx.reshape(-1, 16).T, (8, 1)).astype(np.uint16)


def unstriped(offs):
    return offs[:16].T.reshape(-1).astype(np.int64)


E2M1 = np.array([0.0, 0.5, 1.0, 1.5, 2.0, 3.0, 4.0, 6.0, -0.0, -0.5, -1.0, -1.5, -2.0, -3.0, -4.0, -6.0])


def pack_weight(w, fmt):
    k, n = w.shape
    w = f64(np.asarray(w, np.float32).astype(ml_dtypes.bfloat16)).reshape(k // 32, 32, n)
    amax = np.abs(w).max(1)
    if fmt == "e4m3":
        byte = np.frexp(amax)[1] - 1 + 127 - 7
    else:
        mant, ex = np.frexp(amax / 6.0)
        byte = np.where(mant > 0.5, ex, ex - 1) + 127
    byte = np.clip(np.where(amax > 0, byte, 1), 1, 254)
    scaled = (w * np.exp2(127.0 - byte)[:, None, :]).reshape(k, n).astype(np.float32)
    by_word = np.ascontiguousarray(scaled.reshape(k // 512, 128, 4, n).transpose(0, 1, 3, 2))
    if fmt == "e4m3":
        words = by_word.astype(ml_dtypes.float8_e4m3fn).view(np.uint8)
    else:
        c = by_word.astype(ml_dtypes.float4_e2m1fn).view(np.uint8) & 0xF
        words = (c[..., 0::2] | (c[..., 1::2] << 4)).reshape(k // 512, 128, 2 * n)
    return np.ascontiguousarray(words), np.ascontiguousarray(byte.astype(np.uint8).reshape(k // 512, 16, n))


def unpack_weight(words, scales, fmt):
    g, _, n = scales.shape
    words = np.ascontiguousarray(words).reshape(g, 128, n, -1)
    if fmt == "e4m3":
        vals = words.view(ml_dtypes.float8_e4m3fn).astype(np.float64)
    else:
        nib = np.empty((g, 128, n, 4), np.uint8)
        nib[..., 0::2] = words & 0xF
        nib[..., 1::2] = words >> 4
        vals = E2M1[nib]
    vals = vals * np.repeat(np.exp2(scales.astype(np.float64) - 127.0), 8, axis=1)[..., None]
    return vals.transpose(0, 1, 3, 2).reshape(g * 512, n)


def gelu(v):
    return 0.5 * v * (1.0 + np.tanh(np.sqrt(2.0 / np.pi) * (v + 0.044715 * v**3)))


K, H, T, S, T2, P = 512, 1024, 2048, 512, 1024, 512

def setup_inputs():
    n = np.random.standard_normal
    s = mx_kscale(K)[:, None]
    u = mx_kscale(H)[:, None]
    d = {}
    d["tab_words"], d["tab_scales"] = pack_weight(n((K, T)) * s, "e4m3")
    d["w1"] = (n((K, H)) / s / K ** 0.5).astype(np.float32)
    d["w2_words"], d["w2_scales"] = pack_weight(n((K, H)) / s / K ** 0.5, "e2m1")
    d["w3_words"], d["w3_scales"] = pack_weight(n((K, H)) / s / K ** 0.5, "e4m3")
    d["gain"] = (np.exp(0.3 * n(H)) * u[:, 0]).astype(np.float32)
    d["wgs"] = np.exp(0.3 * n((128, S))).astype(np.float32)
    d["page0"] = (n((H, T2)) * u).astype(np.float32)
    d["ctr"] = (0.5 * n(H) * u[:, 0]).astype(np.float32)
    d["low"] = ((0.4 * n(H) - 0.3) * u[:, 0]).astype(np.float32)
    d["vec"] = (n(H) / u[:, 0] ** 2 / H ** 0.5).astype(np.float32)
    d["cap"] = (0.8 * n((T2, P)) + 0.5).astype(np.float32)
    d["offs"] = striped(np.random.permutation(T)[:S])
    d["offs2"] = striped(np.random.permutation(T2)[:S])
    d["offs3"] = striped(np.random.permutation(T2)[:P])
    return d

def reference(tab_words, tab_scales, w1, w2_words, w2_scales, w3_words, w3_scales, gain, wgs, page0, ctr, low, vec, cap, offs, offs2, offs3):
    v = unpack_weight(tab_words, tab_scales, "e4m3")[:, unstriped(offs)]
    load = mxq(f64(w1), 0, "e4m3").T @ v
    form = unpack_weight(w2_words, w2_scales, "e2m1").T @ v
    rest = unpack_weight(w3_words, w3_scales, "e4m3").T @ v
    h = np.maximum(load * form, rest) * f64(gain)[:, None]
    page = f64(page0).copy()
    page[:, unstriped(offs2)] = np.tile(f64(wgs), (H // 128, 1)) * h
    x = page[:, unstriped(offs3)]
    x = np.maximum(x - f64(ctr)[:, None], f64(low)[:, None]) * f64(vec)[:, None]
    e = mxq(page, 0, "e4m3").T @ mxq(x, 0, "e4m3")
    return np.minimum(e, f64(cap))

@@ -1,0 +1,313 @@
+from contextlib import ExitStack
+
+import concourse.mybir as mybir
+
+K, H, T, S, T2, NP = 512, 1024, 2048, 512, 1024, 512
+FLOPS = 2 * K * H * S * 3 + 2 * H * T2 * NP
+
+F32 = mybir.dt.float32
+BF16 = mybir.dt.bfloat16
+I32 = mybir.dt.int32
+U32 = mybir.dt.uint32
+U16 = mybir.dt.uint16
+U8 = mybir.dt.uint8
+FP8X4 = mybir.dt.float8_e4m3fn_x4
+FP4X4 = mybir.dt.float4_e2m1fn_x4
+ALU = mybir.AluOpType
+COPY = mybir.ActivationFunctionType.Copy
+
+P = 128
+PACK = 4
+PASSES = H // (P * PACK)
+TILES = PASSES * PACK
+BANKS = 8
+W1_SCALAR_COLS = 48
+END_CHUNK = 256
+VECTOR_FROM = 1024
+
+
+def tile_list_socket_fit_scores_kernel(
+    tc, tab_words, tab_scales, w1, w2_words, w2_scales, w3_words, w3_scales, gain, wgs, page0, ctr, low, vec, cap,
+    offs, offs2, offs3, out
+):
+    nc = tc.nc
+    with ExitStack() as ctx:
+        keep = ctx.enter_context(tc.tile_pool(name="keep", bufs=1))
+        ring = ctx.enter_context(tc.tile_pool(name="ring", bufs=3))
+        psum = ctx.enter_context(tc.psum_pool(name="psum", bufs=1))
+
+        def held(name, shape, dtype):
+            return keep.tile(shape, dtype, name=name, align_bytes=64)
+
+        def bank(n):
+            return psum.tile([P, 512], F32, name="bank%d" % (n % BANKS))
+
+        list1 = held("list1", [P, S // 16], U16)
+        list2 = held("list2", [P, S // 16], U16)
+        list3 = held("list3", [P, NP // 16], U16)
+        tab_w = held("tab_w", [P, T], U32)
+        tab_s = held("tab_s", [P, T], U8)
+        v_w = held("v_w", [P, S], U32)
+        v_s = held("v_s", [P, S], U8)
+        w2_raw = held("w2_raw", [P, 2 * H], U8)
+        w3_raw = held("w3_raw", [P, H], U32)
+        ws_raw = held("ws_raw", [P, H], U8)
+        w2_w = held("w2_w", [P, 2 * H], U8)
+        w3_w = held("w3_w", [P, H], U32)
+        ws = held("ws", [P, H], U8)
+        w1_raw = [held("w1_raw%d" % b, [P, PACK, 512], F32) for b in range(PASSES)]
+        w1_bf = [held("w1_bf%d" % b, [P, 512 * PACK], BF16) for b in range(PASSES)]
+        w1_w = [held("w1_w%d" % b, [P, 512], U32) for b in range(PASSES)]
+        w1_s = [held("w1_s%d" % b, [P, 512], U8) for b in range(PASSES)]
+        wgs_sb = held("wgs_sb", [P, PACK * S], F32)
+        cols = {}
+        for name in ("gain", "ctr", "low", "vec"):
+            cols[name] = held(name + "_sb", [P, PASSES, PACK], F32)
+        page = {}
+        staged = [held("staged%d" % n, [P, 2 * T2], F32) for n in range(2)]
+        planes = held("planes", [P, 2 * T2], BF16)
+        x_planes = held("x_planes", [P, 3 * NP], BF16)
+        page_bf = [held("page_bf%d" % b, [P, T2 * PACK], BF16) for b in range(PASSES)]
+        page_w = {}
+        page_s = [held("page_s%d" % b, [P, T2], U8) for b in range(PASSES)]
+        x_bf = [held("x_bf%d" % b, [P, NP * PACK], BF16) for b in range(PASSES)]
+        x_w = [held("x_w%d" % b, [P, NP], U32) for b in range(PASSES)]
+        x_s = [held("x_s%d" % b, [P, NP], U8) for b in range(PASSES)]
+
+        nc.vector.memset(tab_s[:].bitcast(I32), 0)
+        nc.gpsimd.memset(ws_raw[:].bitcast(I32), 0)
+
+        def load_scale_rows(queue, plane_tile, first, src):
+            for q in range(4):
+                queue.dma_start(out=plane_tile[32 * q + first : 32 * q + first + 4, :].bitcast(I32), in_=src[0, 4 * q : 4 * q + 4, :].bitcast(I32))
+
+        def load_col(name, src):
+            nc.sync.dma_start(out=cols[name][:], in_=src.rearrange("(b p t) -> p b t", b=PASSES, t=PACK))
+
+        def load_w1(b):
+            nc.sync.dma_start(out=w1_raw[b][:], in_=w1[:, 512 * b : 512 * (b + 1)].rearrange("(p j) c -> p j c", j=PACK))
+
+        def load_page(i):
+            b, t = divmod(i, PACK)
+            rows = page0[512 * b : 512 * (b + 1), :].rearrange("(p t) m -> p t m", t=PACK)
+            page[i] = ring.tile([P, T2], F32, name="page", bufs=4)
+            nc.sync.dma_start(out=page[i][:], in_=rows[:, t, :])
+
+        load_scale_rows(nc.gpsimd, ws_raw, 4, w3_scales)
+        nc.sync.dma_start(out=list1[:], in_=offs)
+        nc.sync.dma_start(out=list2[:], in_=offs2)
+        nc.sync.dma_start(out=list3[:], in_=offs3)
+        for name, src in (("gain", gain), ("ctr", ctr), ("low", low), ("vec", vec)):
+            load_col(name, src)
+        nc.sync.dma_start(out=tab_w[:].bitcast(I32), in_=tab_words[0].rearrange("p n t -> p (n t)").bitcast(I32))
+        load_scale_rows(nc.sync, tab_s, 0, tab_scales)
+        load_w1(0)
+        nc.sync.dma_start(out=w2_raw[:].bitcast(I32), in_=w2_words[0].bitcast(I32))
+        nc.sync.dma_start(out=w3_raw[:].bitcast(I32), in_=w3_words[0].rearrange("p n t -> p (n t)").bitcast(I32))
+        load_scale_rows(nc.sync, ws_raw, 0, w2_scales)
+        for q in (0, 2, 1, 3):
+            nc.sync.dma_start(out=wgs_sb[32 * q : 32 * (q + 1), :], in_=wgs.rearrange("(p t) j -> p (t j)", t=PACK))
+        load_page(0)
+        load_w1(1)
+        load_page(1)
+        for i in range(2, 4):
+            load_page(i)
+
+        def load_cap(h):
+            nc.sync.dma_start(out=staged[h][:].rearrange("p (u j) -> p u j", j=NP), in_=cap[512 * h : 512 * (h + 1), :].rearrange("(u p) j -> p u j", p=P))
+
+        def deal(dst, src):
+            nc.vector.tensor_copy(
+                out=dst.rearrange("p (b t m) -> p b m t", b=PASSES, t=PACK),
+                in_=src.rearrange("p (b m t) -> p b m t", b=PASSES, t=PACK),
+            )
+
+        nc.vector.tensor_copy(out=v_w[:], in_=tab_w[:].indirect(list1[:]))
+        nc.vector.tensor_copy(out=v_s[:], in_=tab_s[:].indirect(list1[:]))
+
+        def w1_views(b, m0, m1):
+            dst = w1_bf[b][:].rearrange("p (t m j) -> p m j t", t=PACK, j=PACK)[:, m0:m1]
+            src = w1_raw[b][:].rearrange("p j (m t) -> p m j t", t=PACK)[:, m0:m1]
+            return dst, src
+
+        def quantize(codes, scales, values):
+            nc.vector.quantize_mx(out=codes.bitcast(FP8X4), scales=scales, in_=values)
+
+        dst, src = w1_views(0, 0, W1_SCALAR_COLS)
+        nc.scalar.copy(out=dst, in_=src)
+        dst, src = w1_views(0, W1_SCALAR_COLS, P)
+        nc.vector.tensor_copy(out=dst, in_=src)
+        deal(w2_w[:].bitcast(U16), w2_raw[:].bitcast(U16))
+        quantize(w1_w[0][:], w1_s[0][:], w1_bf[0][:])
+        deal(w3_w[:], w3_raw[:])
+        deal(ws[:], ws_raw[:])
+
+        prods = {}
+        hs = {}
+        lfs = {}
+        gws = {}
+
+        def weights(i, gw):
+            b, t = divmod(i, PACK)
+            nc.scalar.activation(out=gw, in_=wgs_sb[:, S * t : S * (t + 1)], func=COPY, scale=cols["gain"][:, b, t : t + 1])
+            gws[i] = gw
+
+        loads = {}
+
+        def load_product(i):
+            b, t = divmod(i, PACK)
+            ct = slice(P * t, P * (t + 1))
+            load = bank(6 + i % 2)
+            nc.tensor.matmul_mx(out=load[:], lhsT=w1_w[b][:, ct].bitcast(FP8X4), lhsT_scale=w1_s[b][:, ct], rhs=v_w[:].bitcast(FP8X4), rhs_scale=v_s[:], start=True, stop=True)
+            loads[i] = held("load%d" % i, [P, S], F32)
+            nc.scalar.copy(out=loads[i][:], in_=load[:])
+
+        def products(i):
+            b, t = divmod(i, PACK)
+            c = slice(P * i, P * (i + 1))
+            ct = slice(P * t, P * (t + 1))
+            form, rest = bank(2 * i % 6), bank(2 * i % 6 + 1)
+            for dst_bank, words, scales in (
+                (form, w2_w[:, 2 * P * i : 2 * P * (i + 1)].bitcast(FP4X4), ws[:, c]),
+                (rest, w3_w[:, c].bitcast(FP8X4), ws[4:P, c]),
+            ):
+                nc.tensor.matmul_mx(out=dst_bank[:], lhsT=words, lhsT_scale=scales, rhs=v_w[:].bitcast(FP8X4), rhs_scale=v_s[:], start=True, stop=True)
+            prods[i] = (loads[i], form, rest)
+            weights(i, held("gw%d" % i, [P, S], F32)[:])
+
+        def h_mult(i):
+            load_sb, form, rest = prods[i]
+            lf = held("turn%d" % (i % 2), [P, S], F32)
+            nc.vector.tensor_tensor(out=lf[:], in0=form[:], in1=load_sb[:], op=ALU.mult)
+            lfs[i] = lf
+
+        def h_max(i):
+            load_sb, form, rest = prods[i]
+            hs[i] = held("h", [P, S], F32)
+            nc.vector.tensor_tensor(out=hs[i][:], in0=rest[:], in1=lfs[i][:], op=ALU.max)
+
+        def scatter(i):
+            nc.vector.tensor_tensor(out=page[i][:].indirect(list2[:]), in0=hs[i][:], in1=gws[i], op=ALU.mult)
+
+        picked = {}
+
+        def gather(i, j0=0, j1=NP):
+            if j0 == 0:
+                picked[i] = held("turn%d" % (i % 2), [P, NP], F32)
+            nc.vector.tensor_copy(out=picked[i][:, j0:j1], in_=page[i][:].indirect(list3[:, j0 // 16 : j1 // 16]))
+
+        def x_make(i, j0=0, j1=NP):
+            b, t = divmod(i, PACK)
+            y = ring.tile([P, j1 - j0], F32, name="y")
+            nc.vector.tensor_scalar(out=y[:], in0=picked[i][:, j0:j1], scalar1=cols["ctr"][:, b, t : t + 1], scalar2=cols["low"][:, b, t : t + 1], op0=ALU.subtract, op1=ALU.max)
+            dst = x_bf[b][:].rearrange("p (j t) -> p j t", t=PACK)[:, j0:j1, t]
+            nc.scalar.activation(out=dst, in_=y[:], func=COPY, scale=cols["vec"][:, b, t : t + 1])
+
+        def stage(i):
+            nc.sync.dma_start(out=staged[i // 2][:, T2 * (i % 2) : T2 * (i % 2 + 1)], in_=page[i][:])
+
+        def plane(i):
+            nc.scalar.copy(out=planes[:, T2 * (i % 2) : T2 * (i % 2 + 1)], in_=page[i][:])
+
+        def weave(n, pair):
+            b, t0 = n // 2, 2 * (n % 2)
+            nc.scalar.copy(
+                out=page_bf[b][:].rearrange("p (c i t) -> p c t i", i=4, t=PACK)[:, :, t0 : t0 + 2, :],
+                in_=pair[:].rearrange("p (t c i) -> p c t i", t=2, i=4),
+            )
+
+        def weave_x():
+            nc.scalar.copy(
+                out=x_bf[1][:].rearrange("p (c i t) -> p c t i", i=4, t=PACK)[:, :, 0:3, :],
+                in_=x_planes[:].rearrange("p (t c i) -> p c t i", t=3, i=4),
+            )
+
+        def one_slot(i, m0, m1):
+            b, t = divmod(i, PACK)
+            dst = page_bf[b][:].rearrange("p (m t) -> p m t", t=PACK)[:, m0:m1, t]
+            if m0 < VECTOR_FROM:
+                nc.scalar.copy(out=dst, in_=page[i][:, m0:m1])
+            else:
+                nc.vector.tensor_copy(out=dst, in_=page[i][:, m0:m1])
+
+        def quantize_page(b, m0, m1):
+            if (b, m0 // 512) not in page_w:
+                slot = "gw7" if (b, m0) == (0, 512) else "page_w%d_%d" % (b, m0 // 512)
+                page_w[b, m0 // 512] = held(slot, [P, 512], U32)
+            quantize(page_w[b, m0 // 512][:, m0 % 512 : m0 % 512 + m1 - m0], page_s[b][:, m0:m1], page_bf[b][:, PACK * m0 : PACK * m1])
+
+        def quantize_x(b, j0, j1):
+            quantize(x_w[b][:, j0:j1], x_s[b][:, j0:j1], x_bf[b][:, PACK * j0 : PACK * j1])
+
+        scores = {}
+
+        def score_pass(u, b, j0, j1):
+            if b == 0:
+                scores[u] = bank((6, 7, 4, 5, 0, 1, 2, 3)[u])
+            m = slice(P * u, P * (u + 1))
+            nc.tensor.matmul_mx(out=scores[u][:, j0:j1], lhsT=page_w[b, u // 4][:, P * (u % 4) : P * (u % 4 + 1)].bitcast(FP8X4), lhsT_scale=page_s[b][:, m], rhs=x_w[b][:, j0:j1].bitcast(FP8X4), rhs_scale=x_s[b][:, j0:j1], start=(b == 0), stop=(b == PASSES - 1 and j1 == NP))
+
+        load_product(0)
+        products(0)
+        load_product(1)
+        products(1)
+        load_product(2)
+        load_product(3)
+        h_mult(0)
+        h_max(0)
+        for i in range(TILES - 1):
+            scatter(i)
+            if i < 4:
+                stage(i)
+            elif i < 6:
+                plane(i)
+            else:
+                one_slot(i, 0, VECTOR_FROM)
+            if i + 2 < TILES:
+                products(i + 2)
+            if i == 0:
+                dst, src = w1_views(1, 0, P)
+                nc.scalar.copy(out=dst, in_=src)
+            h_mult(i + 1)
+            gather(i)
+            if i + 4 < TILES:
+                load_page(i + 4)
+            h_max(i + 1)
+            x_make(i)
+            if i == 0:
+                quantize(w1_w[1][:], w1_s[1][:], w1_bf[1][:])
+                for n in range(PACK, TILES):
+                    load_product(n)
+            if i in (1, 3):
+                weave(i // 2, staged[i // 2])
+                load_cap(i // 2)
+            if i == 5:
+                weave(2, planes)
+                quantize_x(0, 0, NP)
+                quantize_page(0, 0, 512)
+        for u in range(4):
+            score_pass(u, 0, 0, NP)
+        last = TILES - 1
+        half = NP // 2
+        scatter(last)
+        one_slot(last, 0, END_CHUNK)
+        one_slot(last, END_CHUNK, 2 * END_CHUNK)
+        gather(last, 0, half)
+        gather(last, half, NP)
+        x_make(last, 0, half)
+        x_make(last, half, NP)
+        quantize_page(0, 512, T2)
+        for u in range(4, 8):
+            score_pass(u, 0, 0, NP)
+        quantize_page(1, 0, 2 * END_CHUNK)
+        quantize_x(1, 0, half)
+        quantize_x(1, half, NP)
+        for m0 in range(2 * END_CHUNK, T2, END_CHUNK):
+            one_slot(last, m0, m0 + END_CHUNK)
+            quantize_page(1, m0, m0 + END_CHUNK)
+        for u in range(T2 // P):
+            score_pass(u, 1, 0, half)
+            score_pass(u, 1, half, NP)
+            res = held("res%d" % u, [P, NP], F32)
+            nc.vector.tensor_tensor(out=res[:], in0=scores[u][:], in1=staged[u // 4][:, NP * (u % 4) : NP * (u % 4 + 1)], op=ALU.min)
+            nc.sync.dma_start(out=out[P * u : P * (u + 1), :], in_=res[:])

@@ -59,7 +59,8 @@ def tile_list_socket_fit_scores_kernel(
         w1_bf = [held("w1_bf%d" % b, [P, 512 * PACK], BF16) for b in range(PASSES)]
         w1_w = [held("w1_w%d" % b, [P, 512], U32) for b in range(PASSES)]
         w1_s = [held("w1_s%d" % b, [P, 512], U8) for b in range(PASSES)]
-        wgs_sb = held("wgs_sb", [P, PACK * S], F32)
+        wgs_first = held("wgs_first", [P, S], F32)
+        wgs_rest = held("wgs_rest", [P, (PACK - 1) * S], F32)
         cols = {}
         for name in ("gain", "ctr", "low", "vec"):
             cols[name] = held(name + "_sb", [P, PASSES, PACK], F32)
@@ -75,14 +76,18 @@ def tile_list_socket_fit_scores_kernel(
         x_s = [held("x_s%d" % b, [P, NP], U8) for b in range(PASSES)]
 
         nc.vector.memset(tab_s[:].bitcast(I32), 0)
-        nc.gpsimd.memset(ws_raw[:].bitcast(I32), 0)
+        nc.vector.memset(ws_raw[:].bitcast(I32), 0)
 
-        def load_scale_rows(queue, plane_tile, first, src):
-            for q in range(4):
-                queue.dma_start(out=plane_tile[32 * q + first : 32 * q + first + 4, :].bitcast(I32), in_=src[0, 4 * q : 4 * q + 4, :].bitcast(I32))
+        def load_scale_rows(plane_tile, first, src, quadrants):
+            for q in quadrants:
+                nc.sync.dma_start(out=plane_tile[32 * q + first : 32 * q + first + 4, :].bitcast(I32), in_=src[0, 4 * q : 4 * q + 4, :].bitcast(I32))
 
         def load_col(name, src):
             nc.sync.dma_start(out=cols[name][:], in_=src.rearrange("(b p t) -> p b t", b=PASSES, t=PACK))
+
+        def load_wgs(dst, t0, t1):
+            for q in (0, 2, 1, 3):
+                nc.sync.dma_start(out=dst[32 * q : 32 * (q + 1), :], in_=wgs.rearrange("(p t) j -> p (t j)", t=PACK)[:, S * t0 : S * t1])
 
         def load_w1(b):
             nc.sync.dma_start(out=w1_raw[b][:], in_=w1[:, 512 * b : 512 * (b + 1)].rearrange("(p j) c -> p j c", j=PACK))
@@ -93,22 +98,25 @@ def tile_list_socket_fit_scores_kernel(
             page[i] = ring.tile([P, T2], F32, name="page", bufs=4)
             nc.sync.dma_start(out=page[i][:], in_=rows[:, t, :])
 
-        load_scale_rows(nc.gpsimd, ws_raw, 4, w3_scales)
-        nc.sync.dma_start(out=list1[:], in_=offs)
-        nc.sync.dma_start(out=list2[:], in_=offs2)
-        nc.sync.dma_start(out=list3[:], in_=offs3)
-        for name, src in (("gain", gain), ("ctr", ctr), ("low", low), ("vec", vec)):
-            load_col(name, src)
         nc.sync.dma_start(out=tab_w[:].bitcast(I32), in_=tab_words[0].rearrange("p n t -> p (n t)").bitcast(I32))
-        load_scale_rows(nc.sync, tab_s, 0, tab_scales)
+        load_scale_rows(tab_s, 0, tab_scales, range(4))
+        nc.sync.dma_start(out=list1[:], in_=offs)
         load_w1(0)
+        load_scale_rows(ws_raw, 0, w2_scales, range(1))
         nc.sync.dma_start(out=w2_raw[:].bitcast(I32), in_=w2_words[0].bitcast(I32))
         nc.sync.dma_start(out=w3_raw[:].bitcast(I32), in_=w3_words[0].rearrange("p n t -> p (n t)").bitcast(I32))
-        load_scale_rows(nc.sync, ws_raw, 0, w2_scales)
-        for q in (0, 2, 1, 3):
-            nc.sync.dma_start(out=wgs_sb[32 * q : 32 * (q + 1), :], in_=wgs.rearrange("(p t) j -> p (t j)", t=PACK))
+        load_scale_rows(ws_raw, 0, w2_scales, range(1, 4))
+        load_scale_rows(ws_raw, 4, w3_scales, range(4))
+        load_col("gain", gain)
+        load_wgs(wgs_first, 0, 1)
         load_page(0)
+        nc.sync.dma_start(out=list2[:], in_=offs2)
+        nc.sync.dma_start(out=list3[:], in_=offs3)
+        load_col("ctr", ctr)
+        load_col("low", low)
         load_w1(1)
+        load_wgs(wgs_rest, 1, PACK)
+        load_col("vec", vec)
         load_page(1)
         for i in range(2, 4):
             load_page(i)
@@ -116,18 +124,18 @@ def tile_list_socket_fit_scores_kernel(
         def load_cap(h):
             nc.sync.dma_start(out=staged[h][:].rearrange("p (u j) -> p u j", j=NP), in_=cap[512 * h : 512 * (h + 1), :].rearrange("(u p) j -> p u j", p=P))
 
-        def deal(dst, src):
+        def deal(dst, src, line):
             nc.vector.tensor_copy(
-                out=dst.rearrange("p (b t m) -> p b m t", b=PASSES, t=PACK),
-                in_=src.rearrange("p (b m t) -> p b m t", b=PASSES, t=PACK),
+                out=dst.rearrange("p (b t c i) -> p b c t i", b=PASSES, t=PACK, i=line),
+                in_=src.rearrange("p (b c i t) -> p b c t i", b=PASSES, t=PACK, i=line),
             )
 
         nc.vector.tensor_copy(out=v_w[:], in_=tab_w[:].indirect(list1[:]))
         nc.vector.tensor_copy(out=v_s[:], in_=tab_s[:].indirect(list1[:]))
 
         def w1_views(b, m0, m1):
-            dst = w1_bf[b][:].rearrange("p (t m j) -> p m j t", t=PACK, j=PACK)[:, m0:m1]
-            src = w1_raw[b][:].rearrange("p j (m t) -> p m j t", t=PACK)[:, m0:m1]
+            dst = w1_bf[b][:].rearrange("p (t m j) -> p m t j", t=PACK, j=PACK)[:, m0:m1]
+            src = w1_raw[b][:].rearrange("p j (m t) -> p m t j", t=PACK)[:, m0:m1]
             return dst, src
 
         def quantize(codes, scales, values):
@@ -137,10 +145,10 @@ def tile_list_socket_fit_scores_kernel(
         nc.scalar.copy(out=dst, in_=src)
         dst, src = w1_views(0, W1_SCALAR_COLS, P)
         nc.vector.tensor_copy(out=dst, in_=src)
-        deal(w2_w[:].bitcast(U16), w2_raw[:].bitcast(U16))
+        deal(w2_w[:].bitcast(U16), w2_raw[:].bitcast(U16), 8)
         quantize(w1_w[0][:], w1_s[0][:], w1_bf[0][:])
-        deal(w3_w[:], w3_raw[:])
-        deal(ws[:], ws_raw[:])
+        deal(w3_w[:], w3_raw[:], 4)
+        deal(ws[:], ws_raw[:], 16)
 
         prods = {}
         hs = {}
@@ -149,7 +157,7 @@ def tile_list_socket_fit_scores_kernel(
 
         def weights(i, gw):
             b, t = divmod(i, PACK)
-            nc.scalar.activation(out=gw, in_=wgs_sb[:, S * t : S * (t + 1)], func=COPY, scale=cols["gain"][:, b, t : t + 1])
+            nc.scalar.activation(out=gw, in_=(wgs_first[:] if t == 0 else wgs_rest[:, S * (t - 1) : S * t]), func=COPY, scale=cols["gain"][:, b, t : t + 1])
             gws[i] = gw
 
         loads = {}
@@ -212,8 +220,8 @@ def tile_list_socket_fit_scores_kernel(
         def weave(n, pair):
             b, t0 = n // 2, 2 * (n % 2)
             nc.scalar.copy(
-                out=page_bf[b][:].rearrange("p (c i t) -> p c t i", i=4, t=PACK)[:, :, t0 : t0 + 2, :],
-                in_=pair[:].rearrange("p (t c i) -> p c t i", t=2, i=4),
+                out=page_bf[b][:].rearrange("p (m t) -> p m t", t=PACK)[:, :, t0 : t0 + 2],
+                in_=pair[:].rearrange("p (t m) -> p m t", t=2),
             )
 
         def weave_x():

@@ -23,6 +23,8 @@ TILES = PASSES * PACK
 BANKS = 8
 W1_SCALAR_COLS = 48
 END_CHUNK = 256
+REST_BANKS = 3
+ON_VECTOR = 2
 VECTOR_FROM = 1024
 
 
@@ -33,7 +35,6 @@ def tile_list_socket_fit_scores_kernel(
     nc = tc.nc
     with ExitStack() as ctx:
         keep = ctx.enter_context(tc.tile_pool(name="keep", bufs=1))
-        ring = ctx.enter_context(tc.tile_pool(name="ring", bufs=3))
         psum = ctx.enter_context(tc.psum_pool(name="psum", bufs=1))
 
         def held(name, shape, dtype):
@@ -59,15 +60,13 @@ def tile_list_socket_fit_scores_kernel(
         w1_bf = [held("w1_bf%d" % b, [P, 512 * PACK], BF16) for b in range(PASSES)]
         w1_w = [held("w1_w%d" % b, [P, 512], U32) for b in range(PASSES)]
         w1_s = [held("w1_s%d" % b, [P, 512], U8) for b in range(PASSES)]
-        wgs_first = held("wgs_first", [P, S], F32)
-        wgs_rest = held("wgs_rest", [P, (PACK - 1) * S], F32)
+        wgs_sb = {}
         cols = {}
         for name in ("gain", "ctr", "low", "vec"):
             cols[name] = held(name + "_sb", [P, PASSES, PACK], F32)
         page = {}
         staged = [held("staged%d" % n, [P, 2 * T2], F32) for n in range(2)]
         planes = held("planes", [P, 2 * T2], BF16)
-        x_planes = held("x_planes", [P, 3 * NP], BF16)
         page_bf = [held("page_bf%d" % b, [P, T2 * PACK], BF16) for b in range(PASSES)]
         page_w = {}
         page_s = [held("page_s%d" % b, [P, T2], U8) for b in range(PASSES)]
@@ -85,7 +84,10 @@ def tile_list_socket_fit_scores_kernel(
         def load_col(name, src):
             nc.sync.dma_start(out=cols[name][:], in_=src.rearrange("(b p t) -> p b t", b=PASSES, t=PACK))
 
-        def load_wgs(dst, t0, t1):
+        def load_wgs(t0, t1):
+            dst = held("wgs%d" % t0, [P, (t1 - t0) * S], F32)
+            for t in range(t0, t1):
+                wgs_sb[t] = dst[:, S * (t - t0) : S * (t - t0 + 1)]
             for q in (0, 2, 1, 3):
                 nc.sync.dma_start(out=dst[32 * q : 32 * (q + 1), :], in_=wgs.rearrange("(p t) j -> p (t j)", t=PACK)[:, S * t0 : S * t1])
 
@@ -95,31 +97,30 @@ def tile_list_socket_fit_scores_kernel(
         def load_page(i):
             b, t = divmod(i, PACK)
             rows = page0[512 * b : 512 * (b + 1), :].rearrange("(p t) m -> p t m", t=PACK)
-            page[i] = ring.tile([P, T2], F32, name="page", bufs=4)
+            page[i] = held("page%d" % i if i < 2 else "gw%d" % (i - 2), [P, T2], F32)
             nc.sync.dma_start(out=page[i][:], in_=rows[:, t, :])
 
         nc.sync.dma_start(out=tab_w[:].bitcast(I32), in_=tab_words[0].rearrange("p n t -> p (n t)").bitcast(I32))
         load_scale_rows(tab_s, 0, tab_scales, range(4))
         nc.sync.dma_start(out=list1[:], in_=offs)
         load_w1(0)
-        load_scale_rows(ws_raw, 0, w2_scales, range(1))
+        load_scale_rows(ws_raw, 0, w2_scales, range(2))
         nc.sync.dma_start(out=w2_raw[:].bitcast(I32), in_=w2_words[0].bitcast(I32))
         nc.sync.dma_start(out=w3_raw[:].bitcast(I32), in_=w3_words[0].rearrange("p n t -> p (n t)").bitcast(I32))
-        load_scale_rows(ws_raw, 0, w2_scales, range(1, 4))
+        load_scale_rows(ws_raw, 0, w2_scales, range(2, 4))
         load_scale_rows(ws_raw, 4, w3_scales, range(4))
         load_col("gain", gain)
-        load_wgs(wgs_first, 0, 1)
+        load_wgs(0, 1)
         load_page(0)
         nc.sync.dma_start(out=list2[:], in_=offs2)
         nc.sync.dma_start(out=list3[:], in_=offs3)
         load_col("ctr", ctr)
         load_col("low", low)
+        load_wgs(1, 3)
         load_w1(1)
-        load_wgs(wgs_rest, 1, PACK)
-        load_col("vec", vec)
         load_page(1)
-        for i in range(2, 4):
-            load_page(i)
+        load_col("vec", vec)
+        load_wgs(3, 4)
 
         def load_cap(h):
             nc.sync.dma_start(out=staged[h][:].rearrange("p (u j) -> p u j", j=NP), in_=cap[512 * h : 512 * (h + 1), :].rearrange("(u p) j -> p u j", p=P))
@@ -150,49 +151,56 @@ def tile_list_socket_fit_scores_kernel(
         deal(w3_w[:], w3_raw[:], 4)
         deal(ws[:], ws_raw[:], 16)
 
-        prods = {}
         hs = {}
         lfs = {}
         gws = {}
 
         def weights(i, gw):
             b, t = divmod(i, PACK)
-            nc.scalar.activation(out=gw, in_=(wgs_first[:] if t == 0 else wgs_rest[:, S * (t - 1) : S * t]), func=COPY, scale=cols["gain"][:, b, t : t + 1])
+            nc.scalar.activation(out=gw, in_=wgs_sb[t], func=COPY, scale=cols["gain"][:, b, t : t + 1])
             gws[i] = gw
 
         loads = {}
+        forms = {}
+        rests = {}
+        early_uses = []
+
+        def next_early():
+            early_uses.append(0)
+            return REST_BANKS + (len(early_uses) - 1) % (BANKS - REST_BANKS)
+
+        def product(dst_bank, words, scales):
+            nc.tensor.matmul_mx(out=dst_bank[:], lhsT=words, lhsT_scale=scales, rhs=v_w[:].bitcast(FP8X4), rhs_scale=v_s[:], start=True, stop=True)
 
         def load_product(i):
             b, t = divmod(i, PACK)
             ct = slice(P * t, P * (t + 1))
-            load = bank(6 + i % 2)
-            nc.tensor.matmul_mx(out=load[:], lhsT=w1_w[b][:, ct].bitcast(FP8X4), lhsT_scale=w1_s[b][:, ct], rhs=v_w[:].bitcast(FP8X4), rhs_scale=v_s[:], start=True, stop=True)
+            load = bank(next_early())
+            product(load, w1_w[b][:, ct].bitcast(FP8X4), w1_s[b][:, ct])
             loads[i] = held("load%d" % i, [P, S], F32)
             nc.scalar.copy(out=loads[i][:], in_=load[:])
 
-        def products(i):
-            b, t = divmod(i, PACK)
+        def form_product(i, form_all=None):
+            forms[i] = bank(next_early())
+            product(forms[i], w2_w[:, 2 * P * i : 2 * P * (i + 1)].bitcast(FP4X4), ws[:, P * i : P * (i + 1)])
+            if i >= ON_VECTOR:
+                form_sb = form_all[:, S * (i - ON_VECTOR) : S * (i - ON_VECTOR + 1)]
+                nc.scalar.copy(out=form_sb, in_=forms[i][:])
+                forms[i] = form_sb
+
+        def rest_product(i):
             c = slice(P * i, P * (i + 1))
-            ct = slice(P * t, P * (t + 1))
-            form, rest = bank(2 * i % 6), bank(2 * i % 6 + 1)
-            for dst_bank, words, scales in (
-                (form, w2_w[:, 2 * P * i : 2 * P * (i + 1)].bitcast(FP4X4), ws[:, c]),
-                (rest, w3_w[:, c].bitcast(FP8X4), ws[4:P, c]),
-            ):
-                nc.tensor.matmul_mx(out=dst_bank[:], lhsT=words, lhsT_scale=scales, rhs=v_w[:].bitcast(FP8X4), rhs_scale=v_s[:], start=True, stop=True)
-            prods[i] = (loads[i], form, rest)
-            weights(i, held("gw%d" % i, [P, S], F32)[:])
+            rests[i] = bank(i % REST_BANKS)
+            product(rests[i], w3_w[:, c].bitcast(FP8X4), ws[4:P, c])
 
         def h_mult(i):
-            load_sb, form, rest = prods[i]
-            lf = held("turn%d" % (i % 2), [P, S], F32)
-            nc.vector.tensor_tensor(out=lf[:], in0=form[:], in1=load_sb[:], op=ALU.mult)
-            lfs[i] = lf
+            lfs[i] = held("turn%d" % (i % 3), [P, S], F32)
+            engine = nc.vector if i < ON_VECTOR else nc.gpsimd
+            engine.tensor_tensor(out=lfs[i][:], in0=forms[i][:], in1=loads[i][:], op=ALU.mult)
 
         def h_max(i):
-            load_sb, form, rest = prods[i]
             hs[i] = held("h", [P, S], F32)
-            nc.vector.tensor_tensor(out=hs[i][:], in0=rest[:], in1=lfs[i][:], op=ALU.max)
+            nc.vector.tensor_tensor(out=hs[i][:], in0=rests[i][:], in1=lfs[i][:], op=ALU.max)
 
         def scatter(i):
             nc.vector.tensor_tensor(out=page[i][:].indirect(list2[:]), in0=hs[i][:], in1=gws[i], op=ALU.mult)
@@ -201,12 +209,12 @@ def tile_list_socket_fit_scores_kernel(
 
         def gather(i, j0=0, j1=NP):
             if j0 == 0:
-                picked[i] = held("turn%d" % (i % 2), [P, NP], F32)
+                picked[i] = held("turn%d" % (i % 3), [P, NP], F32)
             nc.vector.tensor_copy(out=picked[i][:, j0:j1], in_=page[i][:].indirect(list3[:, j0 // 16 : j1 // 16]))
 
         def x_make(i, j0=0, j1=NP):
             b, t = divmod(i, PACK)
-            y = ring.tile([P, j1 - j0], F32, name="y")
+            y = held("y%d_%d" % (i, j0), [P, j1 - j0], F32)
             nc.vector.tensor_scalar(out=y[:], in0=picked[i][:, j0:j1], scalar1=cols["ctr"][:, b, t : t + 1], scalar2=cols["low"][:, b, t : t + 1], op0=ALU.subtract, op1=ALU.max)
             dst = x_bf[b][:].rearrange("p (j t) -> p j t", t=PACK)[:, j0:j1, t]
             nc.scalar.activation(out=dst, in_=y[:], func=COPY, scale=cols["vec"][:, b, t : t + 1])
@@ -222,12 +230,6 @@ def tile_list_socket_fit_scores_kernel(
             nc.scalar.copy(
                 out=page_bf[b][:].rearrange("p (m t) -> p m t", t=PACK)[:, :, t0 : t0 + 2],
                 in_=pair[:].rearrange("p (t m) -> p m t", t=2),
-            )
-
-        def weave_x():
-            nc.scalar.copy(
-                out=x_bf[1][:].rearrange("p (c i t) -> p c t i", i=4, t=PACK)[:, :, 0:3, :],
-                in_=x_planes[:].rearrange("p (t c i) -> p c t i", t=3, i=4),
             )
 
         def one_slot(i, m0, m1):
@@ -251,46 +253,59 @@ def tile_list_socket_fit_scores_kernel(
 
         def score_pass(u, b, j0, j1):
             if b == 0:
-                scores[u] = bank((6, 7, 4, 5, 0, 1, 2, 3)[u])
+                scores[u] = bank((3, 4, 5, 6, 7, 2, 0, 1)[u])
             m = slice(P * u, P * (u + 1))
             nc.tensor.matmul_mx(out=scores[u][:, j0:j1], lhsT=page_w[b, u // 4][:, P * (u % 4) : P * (u % 4 + 1)].bitcast(FP8X4), lhsT_scale=page_s[b][:, m], rhs=x_w[b][:, j0:j1].bitcast(FP8X4), rhs_scale=x_s[b][:, j0:j1], start=(b == 0), stop=(b == PASSES - 1 and j1 == NP))
 
-        load_product(0)
-        products(0)
-        load_product(1)
-        products(1)
-        load_product(2)
-        load_product(3)
+        for i in range(2):
+            load_product(i)
+            form_product(i)
+            rest_product(i)
         h_mult(0)
+        h_mult(1)
         h_max(0)
+        for i in (0, PACK):
+            weights(i, held("gw%d" % i, [P, S], F32)[:])
+        for i in range(2, PACK):
+            load_product(i)
+        form_all = held("wgs0", [P, (TILES - ON_VECTOR) * S], F32)
+        for i in range(ON_VECTOR, 4):
+            form_product(i, form_all)
+        for i in (1, 2):
+            weights(i, held("gw%d" % i, [P, S], F32)[:])
+        for i in range(4, TILES):
+            form_product(i, form_all)
+        for i in (3, 5, 6, 7):
+            weights(i, held("gw%d" % i, [P, S], F32)[:])
         for i in range(TILES - 1):
             scatter(i)
             if i < 4:
                 stage(i)
             elif i < 6:
                 plane(i)
+                if i == 5:
+                    weave(2, planes)
             else:
                 one_slot(i, 0, VECTOR_FROM)
             if i + 2 < TILES:
-                products(i + 2)
+                load_page(i + 2)
             if i == 0:
                 dst, src = w1_views(1, 0, P)
                 nc.scalar.copy(out=dst, in_=src)
-            h_mult(i + 1)
-            gather(i)
-            if i + 4 < TILES:
-                load_page(i + 4)
-            h_max(i + 1)
-            x_make(i)
-            if i == 0:
                 quantize(w1_w[1][:], w1_s[1][:], w1_bf[1][:])
                 for n in range(PACK, TILES):
                     load_product(n)
+            if i + 2 < TILES:
+                rest_product(i + 2)
+                h_mult(i + 2)
+            gather(i)
+            h_max(i + 1)
+            x_make(i)
             if i in (1, 3):
                 weave(i // 2, staged[i // 2])
-                load_cap(i // 2)
             if i == 5:
-                weave(2, planes)
+                load_cap(0)
+                load_cap(1)
                 quantize_x(0, 0, NP)
                 quantize_page(0, 0, 512)
         for u in range(4):

from contextlib import ExitStack

import concourse.mybir as mybir

K, H, T, S, T2, NP = 512, 1024, 2048, 512, 1024, 512
FLOPS = 2 * K * H * S * 3 + 2 * H * T2 * NP

F32 = mybir.dt.float32
BF16 = mybir.dt.bfloat16
I32 = mybir.dt.int32
U32 = mybir.dt.uint32
U16 = mybir.dt.uint16
U8 = mybir.dt.uint8
FP8X4 = mybir.dt.float8_e4m3fn_x4
FP4X4 = mybir.dt.float4_e2m1fn_x4
ALU = mybir.AluOpType
COPY = mybir.ActivationFunctionType.Copy

P = 128
PACK = 4
PASSES = H // (P * PACK)
TILES = PASSES * PACK
BANKS = 8
W1_SCALAR_COLS = 48
END_CHUNK = 256
REST_BANKS = 3
ON_VECTOR = 2
VECTOR_FROM = 1024


def tile_list_socket_fit_scores_kernel(
    tc, tab_words, tab_scales, w1, w2_words, w2_scales, w3_words, w3_scales, gain, wgs, page0, ctr, low, vec, cap,
    offs, offs2, offs3, out
):
    nc = tc.nc
    with ExitStack() as ctx:
        keep = ctx.enter_context(tc.tile_pool(name="keep", bufs=1))
        psum = ctx.enter_context(tc.psum_pool(name="psum", bufs=1))

        def held(name, shape, dtype):
            return keep.tile(shape, dtype, name=name, align_bytes=64)

        def bank(n):
            return psum.tile([P, 512], F32, name="bank%d" % (n % BANKS))

        list1 = held("list1", [P, S // 16], U16)
        list2 = held("list2", [P, S // 16], U16)
        list3 = held("list3", [P, NP // 16], U16)
        tab_w = held("tab_w", [P, T], U32)
        tab_s = held("tab_s", [P, T], U8)
        v_w = held("v_w", [P, S], U32)
        v_s = held("v_s", [P, S], U8)
        w2_raw = held("w2_raw", [P, 2 * H], U8)
        w3_raw = held("w3_raw", [P, H], U32)
        ws_raw = held("ws_raw", [P, H], U8)
        w2_w = held("w2_w", [P, 2 * H], U8)
        w3_w = held("w3_w", [P, H], U32)
        ws = held("ws", [P, H], U8)
        w1_raw = [held("w1_raw%d" % b, [P, PACK, 512], F32) for b in range(PASSES)]
        w1_bf = [held("w1_bf%d" % b, [P, 512 * PACK], BF16) for b in range(PASSES)]
        w1_w = [held("w1_w%d" % b, [P, 512], U32) for b in range(PASSES)]
        w1_s = [held("w1_s%d" % b, [P, 512], U8) for b in range(PASSES)]
        wgs_sb = {}
        cols = {}
        for name in ("gain", "ctr", "low", "vec"):
            cols[name] = held(name + "_sb", [P, PASSES, PACK], F32)
        page = {}
        staged = [held("staged%d" % n, [P, 2 * T2], F32) for n in range(2)]
        planes = held("planes", [P, 2 * T2], BF16)
        page_bf = [held("page_bf%d" % b, [P, T2 * PACK], BF16) for b in range(PASSES)]
        page_w = {}
        page_s = [held("page_s%d" % b, [P, T2], U8) for b in range(PASSES)]
        x_bf = [held("x_bf%d" % b, [P, NP * PACK], BF16) for b in range(PASSES)]
        x_w = [held("x_w%d" % b, [P, NP], U32) for b in range(PASSES)]
        x_s = [held("x_s%d" % b, [P, NP], U8) for b in range(PASSES)]

        nc.vector.memset(tab_s[:].bitcast(I32), 0)
        nc.vector.memset(ws_raw[:].bitcast(I32), 0)

        def load_scale_rows(plane_tile, first, src, quadrants):
            for q in quadrants:
                nc.sync.dma_start(out=plane_tile[32 * q + first : 32 * q + first + 4, :].bitcast(I32), in_=src[0, 4 * q : 4 * q + 4, :].bitcast(I32))

        def load_col(name, src):
            nc.sync.dma_start(out=cols[name][:], in_=src.rearrange("(b p t) -> p b t", b=PASSES, t=PACK))

        def load_wgs(t0, t1):
            dst = held("wgs%d" % t0, [P, (t1 - t0) * S], F32)
            for t in range(t0, t1):
                wgs_sb[t] = dst[:, S * (t - t0) : S * (t - t0 + 1)]
            for q in (0, 2, 1, 3):
                nc.sync.dma_start(out=dst[32 * q : 32 * (q + 1), :], in_=wgs.rearrange("(p t) j -> p (t j)", t=PACK)[:, S * t0 : S * t1])

        def load_w1(b):
            nc.sync.dma_start(out=w1_raw[b][:], in_=w1[:, 512 * b : 512 * (b + 1)].rearrange("(p j) c -> p j c", j=PACK))

        def load_page(i):
            b, t = divmod(i, PACK)
            rows = page0[512 * b : 512 * (b + 1), :].rearrange("(p t) m -> p t m", t=PACK)
            page[i] = held("page%d" % i if i < 2 else "gw%d" % (i - 2), [P, T2], F32)
            nc.sync.dma_start(out=page[i][:], in_=rows[:, t, :])

        nc.sync.dma_start(out=tab_w[:].bitcast(I32), in_=tab_words[0].rearrange("p n t -> p (n t)").bitcast(I32))
        load_scale_rows(tab_s, 0, tab_scales, range(4))
        nc.sync.dma_start(out=list1[:], in_=offs)
        load_w1(0)
        load_scale_rows(ws_raw, 0, w2_scales, range(2))
        nc.sync.dma_start(out=w2_raw[:].bitcast(I32), in_=w2_words[0].bitcast(I32))
        nc.sync.dma_start(out=w3_raw[:].bitcast(I32), in_=w3_words[0].rearrange("p n t -> p (n t)").bitcast(I32))
        load_scale_rows(ws_raw, 0, w2_scales, range(2, 4))
        load_scale_rows(ws_raw, 4, w3_scales, range(4))
        load_col("gain", gain)
        load_wgs(0, 1)
        load_page(0)
        nc.sync.dma_start(out=list2[:], in_=offs2)
        nc.sync.dma_start(out=list3[:], in_=offs3)
        load_col("ctr", ctr)
        load_col("low", low)
        load_wgs(1, 3)
        load_w1(1)
        load_page(1)
        load_col("vec", vec)
        load_wgs(3, 4)

        def load_cap(h):
            nc.sync.dma_start(out=staged[h][:].rearrange("p (u j) -> p u j", j=NP), in_=cap[512 * h : 512 * (h + 1), :].rearrange("(u p) j -> p u j", p=P))

        def deal(dst, src, line):
            nc.vector.tensor_copy(
                out=dst.rearrange("p (b t c i) -> p b c t i", b=PASSES, t=PACK, i=line),
                in_=src.rearrange("p (b c i t) -> p b c t i", b=PASSES, t=PACK, i=line),
            )

        nc.vector.tensor_copy(out=v_w[:], in_=tab_w[:].indirect(list1[:]))
        nc.vector.tensor_copy(out=v_s[:], in_=tab_s[:].indirect(list1[:]))

        def w1_views(b, m0, m1):
            dst = w1_bf[b][:].rearrange("p (t m j) -> p m t j", t=PACK, j=PACK)[:, m0:m1]
            src = w1_raw[b][:].rearrange("p j (m t) -> p m t j", t=PACK)[:, m0:m1]
            return dst, src

        def quantize(codes, scales, values):
            nc.vector.quantize_mx(out=codes.bitcast(FP8X4), scales=scales, in_=values)

        dst, src = w1_views(0, 0, W1_SCALAR_COLS)
        nc.scalar.copy(out=dst, in_=src)
        dst, src = w1_views(0, W1_SCALAR_COLS, P)
        nc.vector.tensor_copy(out=dst, in_=src)
        deal(w2_w[:].bitcast(U16), w2_raw[:].bitcast(U16), 8)
        quantize(w1_w[0][:], w1_s[0][:], w1_bf[0][:])
        deal(w3_w[:], w3_raw[:], 4)
        deal(ws[:], ws_raw[:], 16)

        hs = {}
        lfs = {}
        gws = {}

        def weights(i, gw):
            b, t = divmod(i, PACK)
            nc.scalar.activation(out=gw, in_=wgs_sb[t], func=COPY, scale=cols["gain"][:, b, t : t + 1])
            gws[i] = gw

        loads = {}
        forms = {}
        rests = {}
        early_uses = []

        def next_early():
            early_uses.append(0)
            return REST_BANKS + (len(early_uses) - 1) % (BANKS - REST_BANKS)

        def product(dst_bank, words, scales):
            nc.tensor.matmul_mx(out=dst_bank[:], lhsT=words, lhsT_scale=scales, rhs=v_w[:].bitcast(FP8X4), rhs_scale=v_s[:], start=True, stop=True)

        def load_product(i):
            b, t = divmod(i, PACK)
            ct = slice(P * t, P * (t + 1))
            load = bank(next_early())
            product(load, w1_w[b][:, ct].bitcast(FP8X4), w1_s[b][:, ct])
            loads[i] = held("load%d" % i, [P, S], F32)
            nc.scalar.copy(out=loads[i][:], in_=load[:])

        def form_product(i, form_all=None):
            forms[i] = bank(next_early())
            product(forms[i], w2_w[:, 2 * P * i : 2 * P * (i + 1)].bitcast(FP4X4), ws[:, P * i : P * (i + 1)])
            if i >= ON_VECTOR:
                form_sb = form_all[:, S * (i - ON_VECTOR) : S * (i - ON_VECTOR + 1)]
                nc.scalar.copy(out=form_sb, in_=forms[i][:])
                forms[i] = form_sb

        def rest_product(i):
            c = slice(P * i, P * (i + 1))
            rests[i] = bank(i % REST_BANKS)
            product(rests[i], w3_w[:, c].bitcast(FP8X4), ws[4:P, c])

        def h_mult(i):
            lfs[i] = held("turn%d" % (i % 3), [P, S], F32)
            engine = nc.vector if i < ON_VECTOR else nc.gpsimd
            engine.tensor_tensor(out=lfs[i][:], in0=forms[i][:], in1=loads[i][:], op=ALU.mult)

        def h_max(i):
            hs[i] = held("h", [P, S], F32)
            nc.vector.tensor_tensor(out=hs[i][:], in0=rests[i][:], in1=lfs[i][:], op=ALU.max)

        def scatter(i):
            nc.vector.tensor_tensor(out=page[i][:].indirect(list2[:]), in0=hs[i][:], in1=gws[i], op=ALU.mult)

        picked = {}

        def gather(i, j0=0, j1=NP):
            if j0 == 0:
                picked[i] = held("turn%d" % (i % 3), [P, NP], F32)
            nc.vector.tensor_copy(out=picked[i][:, j0:j1], in_=page[i][:].indirect(list3[:, j0 // 16 : j1 // 16]))

        def x_make(i, j0=0, j1=NP):
            b, t = divmod(i, PACK)
            y = held("y%d_%d" % (i, j0), [P, j1 - j0], F32)
            nc.vector.tensor_scalar(out=y[:], in0=picked[i][:, j0:j1], scalar1=cols["ctr"][:, b, t : t + 1], scalar2=cols["low"][:, b, t : t + 1], op0=ALU.subtract, op1=ALU.max)
            dst = x_bf[b][:].rearrange("p (j t) -> p j t", t=PACK)[:, j0:j1, t]
            nc.scalar.activation(out=dst, in_=y[:], func=COPY, scale=cols["vec"][:, b, t : t + 1])

        def stage(i):
            nc.sync.dma_start(out=staged[i // 2][:, T2 * (i % 2) : T2 * (i % 2 + 1)], in_=page[i][:])

        def plane(i):
            nc.scalar.copy(out=planes[:, T2 * (i % 2) : T2 * (i % 2 + 1)], in_=page[i][:])

        def weave(n, pair):
            b, t0 = n // 2, 2 * (n % 2)
            nc.scalar.copy(
                out=page_bf[b][:].rearrange("p (m t) -> p m t", t=PACK)[:, :, t0 : t0 + 2],
                in_=pair[:].rearrange("p (t m) -> p m t", t=2),
            )

        def one_slot(i, m0, m1):
            b, t = divmod(i, PACK)
            dst = page_bf[b][:].rearrange("p (m t) -> p m t", t=PACK)[:, m0:m1, t]
            if m0 < VECTOR_FROM:
                nc.scalar.copy(out=dst, in_=page[i][:, m0:m1])
            else:
                nc.vector.tensor_copy(out=dst, in_=page[i][:, m0:m1])

        def quantize_page(b, m0, m1):
            if (b, m0 // 512) not in page_w:
                slot = "gw7" if (b, m0) == (0, 512) else "page_w%d_%d" % (b, m0 // 512)
                page_w[b, m0 // 512] = held(slot, [P, 512], U32)
            quantize(page_w[b, m0 // 512][:, m0 % 512 : m0 % 512 + m1 - m0], page_s[b][:, m0:m1], page_bf[b][:, PACK * m0 : PACK * m1])

        def quantize_x(b, j0, j1):
            quantize(x_w[b][:, j0:j1], x_s[b][:, j0:j1], x_bf[b][:, PACK * j0 : PACK * j1])

        scores = {}

        def score_pass(u, b, j0, j1):
            if b == 0:
                scores[u] = bank((3, 4, 5, 6, 7, 2, 0, 1)[u])
            m = slice(P * u, P * (u + 1))
            nc.tensor.matmul_mx(out=scores[u][:, j0:j1], lhsT=page_w[b, u // 4][:, P * (u % 4) : P * (u % 4 + 1)].bitcast(FP8X4), lhsT_scale=page_s[b][:, m], rhs=x_w[b][:, j0:j1].bitcast(FP8X4), rhs_scale=x_s[b][:, j0:j1], start=(b == 0), stop=(b == PASSES - 1 and j1 == NP))

        for i in range(2):
            load_product(i)
            form_product(i)
            rest_product(i)
        h_mult(0)
        h_mult(1)
        h_max(0)
        for i in (0, PACK):
            weights(i, held("gw%d" % i, [P, S], F32)[:])
        for i in range(2, PACK):
            load_product(i)
        form_all = held("wgs0", [P, (TILES - ON_VECTOR) * S], F32)
        for i in range(ON_VECTOR, 4):
            form_product(i, form_all)
        for i in (1, 2):
            weights(i, held("gw%d" % i, [P, S], F32)[:])
        for i in range(4, TILES):
            form_product(i, form_all)
        for i in (3, 5, 6, 7):
            weights(i, held("gw%d" % i, [P, S], F32)[:])
        for i in range(TILES - 1):
            scatter(i)
            if i < 4:
                stage(i)
            elif i < 6:
                plane(i)
                if i == 5:
                    weave(2, planes)
            else:
                one_slot(i, 0, VECTOR_FROM)
            if i + 2 < TILES:
                load_page(i + 2)
            if i == 0:
                dst, src = w1_views(1, 0, P)
                nc.scalar.copy(out=dst, in_=src)
                quantize(w1_w[1][:], w1_s[1][:], w1_bf[1][:])
                for n in range(PACK, TILES):
                    load_product(n)
            if i + 2 < TILES:
                rest_product(i + 2)
                h_mult(i + 2)
            gather(i)
            h_max(i + 1)
            x_make(i)
            if i in (1, 3):
                weave(i // 2, staged[i // 2])
            if i == 5:
                load_cap(0)
                load_cap(1)
                quantize_x(0, 0, NP)
                quantize_page(0, 0, 512)
        for u in range(4):
            score_pass(u, 0, 0, NP)
        last = TILES - 1
        half = NP // 2
        scatter(last)
        one_slot(last, 0, END_CHUNK)
        one_slot(last, END_CHUNK, 2 * END_CHUNK)
        gather(last, 0, half)
        gather(last, half, NP)
        x_make(last, 0, half)
        x_make(last, half, NP)
        quantize_page(0, 512, T2)
        for u in range(4, 8):
            score_pass(u, 0, 0, NP)
        quantize_page(1, 0, 2 * END_CHUNK)
        quantize_x(1, 0, half)
        quantize_x(1, half, NP)
        for m0 in range(2 * END_CHUNK, T2, END_CHUNK):
            one_slot(last, m0, m0 + END_CHUNK)
            quantize_page(1, m0, m0 + END_CHUNK)
        for u in range(T2 // P):
            score_pass(u, 1, 0, half)
            score_pass(u, 1, half, NP)
            res = held("res%d" % u, [P, NP], F32)
            nc.vector.tensor_tensor(out=res[:], in0=scores[u][:], in1=staged[u // 4][:, NP * (u % 4) : NP * (u % 4 + 1)], op=ALU.min)
            nc.sync.dma_start(out=out[P * u : P * (u + 1), :], in_=res[:])
